import numpy as np
import ml_dtypes


def mxq(x, axis, fmt="e4m3"):
    dtype, down = {"e4m3": (ml_dtypes.float8_e4m3fn, 7), "e5m2": (ml_dtypes.float8_e5m2, 14)}[fmt]
    v = np.moveaxis(np.asarray(x, np.float32).astype(ml_dtypes.bfloat16).astype(np.float64), axis, -1)
    blocks = v.reshape(v.shape[:-1] + (-1, 32))
    amax = np.abs(blocks).max(-1, keepdims=True)
    byte = np.maximum(np.where(amax > 0, np.frexp(amax)[1] - 1 + 127, 0) - down, 1)
    scale = np.exp2(byte - 127.0)
    codes = (blocks / scale).astype(np.float32).astype(dtype).astype(np.float64)
    return np.moveaxis((codes * scale).reshape(v.shape), -1, axis)


WIDE = False


def mx_kscale(k):
    if not WIDE:
        return np.ones(k)
    levels = np.array([10, -10, 5, -5, 0])
    if k % 512:
        return np.exp2(np.random.permutation(np.resize(levels, k // 32))).repeat(32)
    a = np.empty((k // 512, 16))
    for p in range(k // 512):
        a[p, :8] = np.random.permutation(np.resize(levels, 8))
        for g in range(8):
            far = levels[np.abs(levels - a[p, g]) >= 10]
            a[p, g + 8] = far[np.random.randint(len(far))]
    return np.exp2(a.ravel()).repeat(32)


def f64(x):
    return np.asarray(x).astype(np.float64)


def striped(idx):
    return np.tile(idx.reshape(-1, 16).T, (8, 1)).astype(np.uint16)


def unstriped(offs):
    return offs[:16].T.reshape(-1).astype(np.int64)


def pack_weight(w):
    k, n = w.shape
    w = f64(np.asarray(w, np.float32).astype(ml_dtypes.bfloat16)).reshape(k // 32, 32, n)
    amax = np.abs(w).max(1)
    byte = np.clip(np.where(amax > 0, np.frexp(amax)[1] - 1 + 127 - 7, 1), 1, 254)
    scaled = (w * np.exp2(127.0 - byte)[:, None, :]).reshape(k, n).astype(np.float32)
    words = np.ascontiguousarray(scaled.reshape(k // 512, 128, 4, n).transpose(0, 1, 3, 2)).astype(ml_dtypes.float8_e4m3fn).view(np.uint8)
    return words, np.ascontiguousarray(byte.astype(np.uint8).reshape(k // 512, 16, n))


def unpack_weight(words, scales):
    g, p, n, _ = words.shape
    vals = np.ascontiguousarray(words).view(ml_dtypes.float8_e4m3fn).astype(np.float64) * np.repeat(np.exp2(scales.astype(np.float64) - 127.0), 8, axis=1)[..., None]
    return vals.transpose(0, 1, 3, 2).reshape(g * 512, n)


E2M1 = np.array([0.0, 0.5, 1.0, 1.5, 2.0, 3.0, 4.0, 6.0, -0.0, -0.5, -1.0, -1.5, -2.0, -3.0, -4.0, -6.0])


def pack_fp4(w):
    k, n = w.shape
    w = f64(np.asarray(w, np.float32).astype(ml_dtypes.bfloat16)).reshape(k // 32, 32, n)
    amax = np.abs(w).max(1)
    mant, ex = np.frexp(amax / 6.0)
    byte = np.clip(np.where(amax > 0, np.where(mant > 0.5, ex, ex - 1) + 127, 1), 1, 254)
    scaled = (w * np.exp2(127.0 - byte)[:, None, :]).reshape(k, n).astype(np.float32)
    c = np.ascontiguousarray(scaled.reshape(k // 512, 128, 4, n).transpose(0, 1, 3, 2)).astype(ml_dtypes.float4_e2m1fn).view(np.uint8) & 0xF
    words = (c[..., 0::2] | (c[..., 1::2] << 4)).reshape(k // 512, 128, 2 * n)
    return np.ascontiguousarray(words), np.ascontiguousarray(byte.astype(np.uint8).reshape(k // 512, 16, n))


def unpack_fp4(words, scales):
    g, _, n = scales.shape
    words = np.ascontiguousarray(words).reshape(g, 128, n, 2)
    nib = np.empty((g, 128, n, 4), np.uint8)
    nib[..., 0::2] = words & 0xF
    nib[..., 1::2] = words >> 4
    vals = E2M1[nib] * np.repeat(np.exp2(scales.astype(np.float64) - 127.0), 8, axis=1)[..., None]
    return vals.transpose(0, 1, 3, 2).reshape(g * 512, n)


K, T, S, H, N = 512, 2048, 1024, 512, 256


def setup_inputs():
    n = np.random.standard_normal
    s = mx_kscale(K)[:, None]
    u = mx_kscale(H)
    packed_xT = pack_weight(n((K, T)) * s)
    packed_w1 = pack_fp4(n((K, N)) / np.sqrt(2 * K) / s)
    packed_w3 = pack_fp4(n((H, N)) / np.sqrt(2 * H) / u[:, None])
    return {
        "x_words": packed_xT[0],
        "x_scales": packed_xT[1],
        "w1_words": packed_w1[0],
        "w1_scales": packed_w1[1],
        "w2": (n((K, H)) / np.sqrt(K) / s * u).astype(np.float32),
        "w3_words": packed_w3[0],
        "w3_scales": packed_w3[1],
        "offs": striped(np.random.permutation(T)[:S]),
    }


def reference(x_words, x_scales, w1_words, w1_scales, w2, w3_words, w3_scales, offs):
    xq = unpack_weight(x_words, x_scales)[:, unstriped(offs)]
    h = mxq(f64(w2), 0, "e4m3").T @ xq
    return unpack_fp4(w1_words, w1_scales).T @ xq + unpack_fp4(w3_words, w3_scales).T @ mxq(h, 0, "e4m3")

@@ -1,0 +1,134 @@
+from contextlib import ExitStack
+
+import concourse.mybir as mybir
+
+K, T, S, H, N = 512, 2048, 1024, 512, 256
+FLOPS = 2 * S * (K * H + K * N + H * N)
+
+F32 = mybir.dt.float32
+BF16 = mybir.dt.bfloat16
+I32 = mybir.dt.int32
+U32 = mybir.dt.uint32
+U16 = mybir.dt.uint16
+U8 = mybir.dt.uint8
+FP8X4 = mybir.dt.float8_e4m3fn_x4
+FP4X4 = mybir.dt.float4_e2m1fn_x4
+P = 128
+
+
+def tile_picked_lora_none_p_kernel(tc, x_words, x_scales, w1_words, w1_scales, w2, w3_words, w3_scales, offs, out):
+    nc = tc.nc
+    with ExitStack() as ctx:
+        keep = ctx.enter_context(tc.tile_pool(name="keep", bufs=1))
+        hps = ctx.enter_context(tc.psum_pool(name="hps", bufs=4))
+        ops = ctx.enter_context(tc.psum_pool(name="ops", bufs=1))
+
+        offsets = keep.tile([P, S // 16], U16, name="offsets")
+        nc.sync.dma_start(offsets[:], offs)
+
+        xs = keep.tile([P, T], U8, name="xs", align_bytes=64)
+        nc.vector.memset(xs[:].bitcast(I32), 0)
+        ws = keep.tile([P, 2 * N], U8, name="ws", align_bytes=64)
+        nc.vector.memset(ws[:].bitcast(I32), 0)
+        for q in range(4):
+            nc.scalar.dma_start(out=xs[32 * q : 32 * q + 4, :].bitcast(I32), in_=x_scales[0, 4 * q : 4 * q + 4, :].bitcast(I32))
+
+        w2raw = keep.tile([P, 4, H], F32, name="w2raw")
+        nc.sync.dma_start(out=w2raw[:], in_=w2.rearrange("(p j) c -> p j c", j=4))
+        xw = keep.tile([P, T], I32, name="xw", align_bytes=64)
+        nc.sync.dma_start(out=xw[:], in_=x_words[0].rearrange("p n t -> p (n t)").bitcast(I32))
+
+        w1w = keep.tile([P, 2 * N], U8, name="w1w", align_bytes=64)
+        w3w = keep.tile([P, 2 * N], U8, name="w3w", align_bytes=64)
+        nc.gpsimd.dma_start(out=w1w[:].bitcast(I32), in_=w1_words[0].bitcast(I32))
+        nc.gpsimd.dma_start(out=w3w[:].bitcast(I32), in_=w3_words[0].bitcast(I32))
+        for a, sc in enumerate((w1_scales, w3_scales)):
+            for q in range(4):
+                nc.sync.dma_start(out=ws[32 * q : 32 * q + 4, a * N : (a + 1) * N].bitcast(I32), in_=sc[0, 4 * q : 4 * q + 4, :].bitcast(I32))
+
+        gs = keep.tile([P, S], U8, name="gs", align_bytes=64)
+        nc.vector.tensor_copy(gs[:], xs[:].indirect(offsets[:]))
+
+        w2b = keep.tile([P, 4, P, 4], BF16, name="w2b", align_bytes=64)
+        src = w2raw[:].rearrange("p j (m t) -> p m j t", t=4)
+        dst = w2b[:].rearrange("p t m j -> p m j t")
+        MS = 80
+        nc.scalar.copy(out=dst[:, :MS], in_=src[:, :MS])
+        nc.vector.tensor_copy(out=dst[:, MS:], in_=src[:, MS:])
+        w2q = keep.tile([P, H], U32, name="w2q", align_bytes=64)
+        w2s = keep.tile([P, H], U8, name="w2s", align_bytes=64)
+        nc.vector.quantize_mx(out=w2q[:].bitcast(FP8X4), scales=w2s[:], in_=w2b[:].rearrange("p t m j -> p (t m j)"))
+
+        gw = keep.tile([P, S], U32, name="gw", align_bytes=64)
+        for g in range(4):
+            nc.vector.tensor_copy(gw[:, 256 * g : 256 * (g + 1)], xw[:].bitcast(U32).indirect(offsets[:, 16 * g : 16 * (g + 1)]))
+
+        hb = keep.tile([P, S * 4], BF16, name="hb", align_bytes=64)
+        hq = keep.tile([P, S], U32, name="hq", align_bytes=64)
+        hs = keep.tile([P, S], U8, name="hs", align_bytes=64)
+        outv = out.rearrange("(a p) n -> p a n", p=P)
+
+        def copy(eng, dst, src):
+            if eng == "s":
+                nc.scalar.copy(out=dst, in_=src)
+            else:
+                nc.vector.tensor_copy(out=dst, in_=src)
+
+        def hidden(c, eng):
+            cols = slice(P * c, P * (c + 1))
+            bank = hps.tile([P, 4, P], F32, name="hbank")
+            for t in range(4):
+                nc.tensor.matmul_mx(out=bank[:, t, :], lhsT=w2q[:, P * t : P * (t + 1)].bitcast(FP8X4), lhsT_scale=w2s[:, P * t : P * (t + 1)],
+                                    rhs=gw[:, cols].bitcast(FP8X4), rhs_scale=gs[:, cols], start=True, stop=True)
+            copy(eng, hb[:, 4 * P * c : 4 * P * (c + 1)].rearrange("p (n t) -> p n t", t=4), bank[:].rearrange("p t n -> p n t"))
+
+        def quant(c0, c1):
+            cols = slice(P * c0, P * c1)
+            nc.vector.quantize_mx(out=hq[:, cols].bitcast(FP8X4), scales=hs[:, cols], in_=hb[:, 4 * P * c0 : 4 * P * c1])
+
+        def own(dst, a, cols):
+            nc.tensor.matmul_mx(out=dst, lhsT=w1w[:, 2 * P * a : 2 * P * (a + 1)].bitcast(FP4X4), lhsT_scale=ws[:, P * a : P * (a + 1)],
+                                rhs=gw[:, cols].bitcast(FP8X4), rhs_scale=gs[:, cols], start=True, stop=False)
+
+        def adapter(dst, a, cols):
+            nc.tensor.matmul_mx(out=dst, lhsT=w3w[:, 2 * P * a : 2 * P * (a + 1)].bitcast(FP4X4), lhsT_scale=ws[:, N + P * a : N + P * (a + 1)],
+                                rhs=hq[:, cols].bitcast(FP8X4), rhs_scale=hs[:, cols], start=False, stop=True)
+
+        def narrow(c0, c1, eng, bank, name):
+            w = P * (c1 - c0)
+            for c in range(c0, c1):
+                for a in range(2):
+                    dst = bank[:, a * w + P * (c - c0) : a * w + P * (c - c0 + 1)]
+                    own(dst, a, slice(P * c, P * (c + 1)))
+                    adapter(dst, a, slice(P * c, P * (c + 1)))
+            res = keep.tile([P, 2 * w], F32, name=name)
+            copy(eng, res[:], bank[:, : 2 * w])
+            nc.sync.dma_start(out=outv[:, :, P * c0 : P * c1], in_=res[:].rearrange("p (a n) -> p a n", a=2))
+
+        wide = [ops.tile([P, 512], F32, name=f"wide{a}") for a in range(2)]
+        ob = ops.tile([P, 512], F32, name="ob")
+        oc = ops.tile([P, 512], F32, name="oc")
+        half = slice(0, 512)
+        for c in range(4):
+            hidden(c, "s")
+        quant(0, 2)
+        hidden(4, "v")
+        for a in range(2):
+            own(wide[a][:], a, half)
+        quant(2, 4)
+        hidden(5, "s")
+        hidden(6, "v")
+        for a in range(2):
+            adapter(wide[a][:], a, half)
+        for a, eng in enumerate("sv"):
+            res = keep.tile([P, 512], F32, name=f"res{a}")
+            copy(eng, res[:], wide[a][:])
+            nc.sync.dma_start(out=outv[:, a, half], in_=res[:])
+        hidden(7, "s")
+        quant(4, 6)
+        quant(6, 7)
+        narrow(4, 6, "s", ob, "resb")
+        quant(7, 8)
+        narrow(6, 7, "v", oc, "resc")
+        od = hps.tile([P, 512], F32, name="hbank")
+        narrow(7, 8, "s", od, "resd")

@@ -26,42 +26,41 @@ def tile_picked_lora_none_p_kernel(tc, x_words, x_scales, w1_words, w1_scales, w
         offsets = keep.tile([P, S // 16], U16, name="offsets")
         nc.sync.dma_start(offsets[:], offs)
 
+        w2v = w2.rearrange("(p j) c -> p j c", j=4)
+        w2raw = [keep.tile([P, 4, H // 2], F32, name=f"w2raw{u}") for u in range(2)]
+        nc.sync.dma_start(out=w2raw[0][:], in_=w2v[:, :, : H // 2])
+        w1w = keep.tile([P, 2 * N], U8, name="w1w", align_bytes=64)
+        w3w = keep.tile([P, 2 * N], U8, name="w3w", align_bytes=64)
+        nc.sync.dma_start(out=w1w[:].bitcast(I32), in_=w1_words[0].bitcast(I32))
         xs = keep.tile([P, T], U8, name="xs", align_bytes=64)
         nc.vector.memset(xs[:].bitcast(I32), 0)
         ws = keep.tile([P, 2 * N], U8, name="ws", align_bytes=64)
         nc.vector.memset(ws[:].bitcast(I32), 0)
         for q in range(4):
-            nc.scalar.dma_start(out=xs[32 * q : 32 * q + 4, :].bitcast(I32), in_=x_scales[0, 4 * q : 4 * q + 4, :].bitcast(I32))
-
-        w2raw = keep.tile([P, 4, H], F32, name="w2raw")
-        nc.sync.dma_start(out=w2raw[:], in_=w2.rearrange("(p j) c -> p j c", j=4))
+            nc.sync.dma_start(out=xs[32 * q : 32 * q + 4, :].bitcast(I32), in_=x_scales[0, 4 * q : 4 * q + 4, :].bitcast(I32))
         xw = keep.tile([P, T], I32, name="xw", align_bytes=64)
         nc.sync.dma_start(out=xw[:], in_=x_words[0].rearrange("p n t -> p (n t)").bitcast(I32))
-
-        w1w = keep.tile([P, 2 * N], U8, name="w1w", align_bytes=64)
-        w3w = keep.tile([P, 2 * N], U8, name="w3w", align_bytes=64)
-        nc.gpsimd.dma_start(out=w1w[:].bitcast(I32), in_=w1_words[0].bitcast(I32))
-        nc.gpsimd.dma_start(out=w3w[:].bitcast(I32), in_=w3_words[0].bitcast(I32))
-        for a, sc in enumerate((w1_scales, w3_scales)):
-            for q in range(4):
-                nc.sync.dma_start(out=ws[32 * q : 32 * q + 4, a * N : (a + 1) * N].bitcast(I32), in_=sc[0, 4 * q : 4 * q + 4, :].bitcast(I32))
+        for q in range(4):
+            nc.sync.dma_start(out=ws[32 * q : 32 * q + 4, :N].bitcast(I32), in_=w1_scales[0, 4 * q : 4 * q + 4, :].bitcast(I32))
+        nc.sync.dma_start(out=w2raw[1][:], in_=w2v[:, :, H // 2 :])
+        nc.sync.dma_start(out=w3w[:].bitcast(I32), in_=w3_words[0].bitcast(I32))
+        for q in range(4):
+            nc.sync.dma_start(out=ws[32 * q : 32 * q + 4, N:].bitcast(I32), in_=w3_scales[0, 4 * q : 4 * q + 4, :].bitcast(I32))
 
         gs = keep.tile([P, S], U8, name="gs", align_bytes=64)
         nc.vector.tensor_copy(gs[:], xs[:].indirect(offsets[:]))
 
-        w2b = keep.tile([P, 4, P, 4], BF16, name="w2b", align_bytes=64)
-        src = w2raw[:].rearrange("p j (m t) -> p m j t", t=4)
-        dst = w2b[:].rearrange("p t m j -> p m j t")
-        MS = 80
-        nc.scalar.copy(out=dst[:, :MS], in_=src[:, :MS])
-        nc.vector.tensor_copy(out=dst[:, MS:], in_=src[:, MS:])
-        w2q = keep.tile([P, H], U32, name="w2q", align_bytes=64)
-        w2s = keep.tile([P, H], U8, name="w2s", align_bytes=64)
-        nc.vector.quantize_mx(out=w2q[:].bitcast(FP8X4), scales=w2s[:], in_=w2b[:].rearrange("p t m j -> p (t m j)"))
-
         gw = keep.tile([P, S], U32, name="gw", align_bytes=64)
         for g in range(4):
             nc.vector.tensor_copy(gw[:, 256 * g : 256 * (g + 1)], xw[:].bitcast(U32).indirect(offsets[:, 16 * g : 16 * (g + 1)]))
+
+        w2b = keep.tile([P, 4, P, 4], BF16, name="w2b", align_bytes=64)
+        dst = w2b[:].rearrange("p t m j -> p m j t")
+        for u in range(2):
+            nc.scalar.copy(out=dst[:, 64 * u : 64 * (u + 1)], in_=w2raw[u][:].rearrange("p j (m t) -> p m j t", t=4))
+        w2q = keep.tile([P, H], U32, name="w2q", align_bytes=64)
+        w2s = keep.tile([P, H], U8, name="w2s", align_bytes=64)
+        nc.vector.quantize_mx(out=w2q[:].bitcast(FP8X4), scales=w2s[:], in_=w2b[:].rearrange("p t m j -> p (t m j)"))
 
         hb = keep.tile([P, S * 4], BF16, name="hb", align_bytes=64)
         hq = keep.tile([P, S], U32, name="hq", align_bytes=64)
@@ -86,49 +85,54 @@ def tile_picked_lora_none_p_kernel(tc, x_words, x_scales, w1_words, w1_scales, w
             cols = slice(P * c0, P * c1)
             nc.vector.quantize_mx(out=hq[:, cols].bitcast(FP8X4), scales=hs[:, cols], in_=hb[:, 4 * P * c0 : 4 * P * c1])
 
-        def own(dst, a, cols):
+        def own(dst, a, cols, start):
             nc.tensor.matmul_mx(out=dst, lhsT=w1w[:, 2 * P * a : 2 * P * (a + 1)].bitcast(FP4X4), lhsT_scale=ws[:, P * a : P * (a + 1)],
-                                rhs=gw[:, cols].bitcast(FP8X4), rhs_scale=gs[:, cols], start=True, stop=False)
+                                rhs=gw[:, cols].bitcast(FP8X4), rhs_scale=gs[:, cols], start=start, stop=False)
 
-        def adapter(dst, a, cols):
+        def adapter(dst, a, cols, stop):
             nc.tensor.matmul_mx(out=dst, lhsT=w3w[:, 2 * P * a : 2 * P * (a + 1)].bitcast(FP4X4), lhsT_scale=ws[:, N + P * a : N + P * (a + 1)],
-                                rhs=hq[:, cols].bitcast(FP8X4), rhs_scale=hs[:, cols], start=False, stop=True)
+                                rhs=hq[:, cols].bitcast(FP8X4), rhs_scale=hs[:, cols], start=False, stop=stop)
 
-        def narrow(c0, c1, eng, bank, name):
+        def narrow(fn, c0, c1, bank):
             w = P * (c1 - c0)
             for c in range(c0, c1):
                 for a in range(2):
                     dst = bank[:, a * w + P * (c - c0) : a * w + P * (c - c0 + 1)]
-                    own(dst, a, slice(P * c, P * (c + 1)))
-                    adapter(dst, a, slice(P * c, P * (c + 1)))
+                    edge = (c == c0 and a == 0) if fn is own else (c == c1 - 1 and a == 1)
+                    fn(dst, a, slice(P * c, P * (c + 1)), edge)
+
+        def leave(c0, c1, eng, bank, name):
+            w = P * (c1 - c0)
             res = keep.tile([P, 2 * w], F32, name=name)
             copy(eng, res[:], bank[:, : 2 * w])
             nc.sync.dma_start(out=outv[:, :, P * c0 : P * c1], in_=res[:].rearrange("p (a n) -> p a n", a=2))
 
-        wide = [ops.tile([P, 512], F32, name=f"wide{a}") for a in range(2)]
-        ob = ops.tile([P, 512], F32, name="ob")
-        oc = ops.tile([P, 512], F32, name="oc")
-        half = slice(0, 512)
-        for c in range(4):
-            hidden(c, "s")
+        obank = [ops.tile([P, 512], F32, name=f"obank{g}") for g in range(4)]
+        spans = [(0, 2), (2, 4), (4, 6), (6, 7)]
+        for g in range(4):
+            narrow(own, spans[g][0], spans[g][1], obank[g])
+        hidden(0, "s")
+        hidden(1, "v")
+        hidden(2, "s")
+        hidden(3, "v")
         quant(0, 2)
-        hidden(4, "v")
-        for a in range(2):
-            own(wide[a][:], a, half)
-        quant(2, 4)
+        hidden(4, "s")
         hidden(5, "s")
+        quant(2, 4)
+        narrow(adapter, 0, 2, obank[0])
         hidden(6, "v")
-        for a in range(2):
-            adapter(wide[a][:], a, half)
-        for a, eng in enumerate("sv"):
-            res = keep.tile([P, 512], F32, name=f"res{a}")
-            copy(eng, res[:], wide[a][:])
-            nc.sync.dma_start(out=outv[:, a, half], in_=res[:])
         hidden(7, "s")
+        narrow(adapter, 2, 4, obank[1])
+        last = hps.tile([P, 512], F32, name="hbank")
+        narrow(own, 7, 8, last)
         quant(4, 6)
+        leave(0, 2, "s", obank[0], "res0")
         quant(6, 7)
-        narrow(4, 6, "s", ob, "resb")
         quant(7, 8)
-        narrow(6, 7, "v", oc, "resc")
-        od = hps.tile([P, 512], F32, name="hbank")
-        narrow(7, 8, "s", od, "resd")
+        narrow(adapter, 4, 6, obank[2])
+        narrow(adapter, 6, 7, obank[3])
+        narrow(adapter, 7, 8, last)
+        leave(2, 4, "v", obank[1], "res1")
+        leave(4, 6, "s", obank[2], "res2")
+        leave(6, 7, "v", obank[3], "res3")
+        leave(7, 8, "v", last, "res4")

@@ -20,7 +20,7 @@ def tile_picked_lora_none_p_kernel(tc, x_words, x_scales, w1_words, w1_scales, w
     nc = tc.nc
     with ExitStack() as ctx:
         keep = ctx.enter_context(tc.tile_pool(name="keep", bufs=1))
-        hps = ctx.enter_context(tc.psum_pool(name="hps", bufs=4))
+        hps = ctx.enter_context(tc.psum_pool(name="hps", bufs=5))
         ops = ctx.enter_context(tc.psum_pool(name="ops", bufs=1))
 
         offsets = keep.tile([P, S // 16], U16, name="offsets")
@@ -29,38 +29,50 @@ def tile_picked_lora_none_p_kernel(tc, x_words, x_scales, w1_words, w1_scales, w
         w2v = w2.rearrange("(p j) c -> p j c", j=4)
         w2raw = [keep.tile([P, 4, H // 2], F32, name=f"w2raw{u}") for u in range(2)]
         nc.sync.dma_start(out=w2raw[0][:], in_=w2v[:, :, : H // 2])
-        w1w = keep.tile([P, 2 * N], U8, name="w1w", align_bytes=64)
-        w3w = keep.tile([P, 2 * N], U8, name="w3w", align_bytes=64)
-        nc.sync.dma_start(out=w1w[:].bitcast(I32), in_=w1_words[0].bitcast(I32))
-        xs = keep.tile([P, T], U8, name="xs", align_bytes=64)
+        xs = keep.tile([P, T], U8, name="xs", tag="xs", align_bytes=64)
         nc.vector.memset(xs[:].bitcast(I32), 0)
         ws = keep.tile([P, 2 * N], U8, name="ws", align_bytes=64)
         nc.vector.memset(ws[:].bitcast(I32), 0)
         for q in range(4):
             nc.sync.dma_start(out=xs[32 * q : 32 * q + 4, :].bitcast(I32), in_=x_scales[0, 4 * q : 4 * q + 4, :].bitcast(I32))
+        nc.sync.dma_start(out=w2raw[1][:], in_=w2v[:, :, H // 2 :])
         xw = keep.tile([P, T], I32, name="xw", align_bytes=64)
         nc.sync.dma_start(out=xw[:], in_=x_words[0].rearrange("p n t -> p (n t)").bitcast(I32))
-        for q in range(4):
-            nc.sync.dma_start(out=ws[32 * q : 32 * q + 4, :N].bitcast(I32), in_=w1_scales[0, 4 * q : 4 * q + 4, :].bitcast(I32))
-        nc.sync.dma_start(out=w2raw[1][:], in_=w2v[:, :, H // 2 :])
-        nc.sync.dma_start(out=w3w[:].bitcast(I32), in_=w3_words[0].bitcast(I32))
-        for q in range(4):
-            nc.sync.dma_start(out=ws[32 * q : 32 * q + 4, N:].bitcast(I32), in_=w3_scales[0, 4 * q : 4 * q + 4, :].bitcast(I32))
+        w1w = keep.tile([P, 2 * N], U8, name="w1w", align_bytes=64)
+        w3w = keep.tile([P, 2 * N], U8, name="w3w", align_bytes=64)
+        for a, (wt, wd, sc) in enumerate(((w1w, w1_words, w1_scales), (w3w, w3_words, w3_scales))):
+            nc.sync.dma_start(out=wt[:].bitcast(I32), in_=wd[0].bitcast(I32))
+            for q in range(4):
+                nc.sync.dma_start(out=ws[32 * q : 32 * q + 4, a * N : (a + 1) * N].bitcast(I32), in_=sc[0, 4 * q : 4 * q + 4, :].bitcast(I32))
+
+        zb = keep.tile([P, 4 * 512], BF16, name="zb", align_bytes=64)
+        nc.vector.memset(zb[:].bitcast(I32), 0)
+        zq = keep.tile([P, 512], U32, name="zq", align_bytes=64)
+        zs = keep.tile([P, 512], U8, name="zs", align_bytes=64)
+        nc.vector.quantize_mx(out=zq[:].bitcast(FP8X4), scales=zs[:], in_=zb[:])
 
         gs = keep.tile([P, S], U8, name="gs", align_bytes=64)
-        nc.vector.tensor_copy(gs[:], xs[:].indirect(offsets[:]))
+        for u in range(2):
+            nc.vector.tensor_copy(gs[:, 512 * u : 512 * (u + 1)], xs[:].indirect(offsets[:, 32 * u : 32 * (u + 1)]))
+        for u in range(4):
+            warm = hps.tile([P, 512], F32, name="hbank")
+            nc.tensor.matmul_mx(out=warm[:], lhsT=zq[:, :P].bitcast(FP8X4), lhsT_scale=zs[:, :P],
+                                rhs=zq[:].bitcast(FP8X4), rhs_scale=gs[:, :512], start=True, stop=True)
 
-        gw = keep.tile([P, S], U32, name="gw", align_bytes=64)
-        for g in range(4):
-            nc.vector.tensor_copy(gw[:, 256 * g : 256 * (g + 1)], xw[:].bitcast(U32).indirect(offsets[:, 16 * g : 16 * (g + 1)]))
-
-        w2b = keep.tile([P, 4, P, 4], BF16, name="w2b", align_bytes=64)
+        w2b = keep.tile([P, 4, P, 4], BF16, name="w2b", tag="w2b", align_bytes=64)
         dst = w2b[:].rearrange("p t m j -> p m j t")
         for u in range(2):
             nc.scalar.copy(out=dst[:, 64 * u : 64 * (u + 1)], in_=w2raw[u][:].rearrange("p j (m t) -> p m j t", t=4))
-        w2q = keep.tile([P, H], U32, name="w2q", align_bytes=64)
+        w2q = keep.tile([P, H], U32, name="w2q", tag="xs", align_bytes=64)
         w2s = keep.tile([P, H], U8, name="w2s", align_bytes=64)
         nc.vector.quantize_mx(out=w2q[:].bitcast(FP8X4), scales=w2s[:], in_=w2b[:].rearrange("p t m j -> p (t m j)"))
+
+        gw = keep.tile([P, S], U32, name="gw", tag="w2b", align_bytes=64)
+        for g in range(4):
+            nc.vector.tensor_copy(gw[:, 256 * g : 256 * (g + 1)], xw[:].bitcast(U32).indirect(offsets[:, 16 * g : 16 * (g + 1)]))
+
+        def picked(cols):
+            return gw[:, cols].bitcast(FP8X4)
 
         hb = keep.tile([P, S * 4], BF16, name="hb", align_bytes=64)
         hq = keep.tile([P, S], U32, name="hq", align_bytes=64)
@@ -78,7 +90,7 @@ def tile_picked_lora_none_p_kernel(tc, x_words, x_scales, w1_words, w1_scales, w
             bank = hps.tile([P, 4, P], F32, name="hbank")
             for t in range(4):
                 nc.tensor.matmul_mx(out=bank[:, t, :], lhsT=w2q[:, P * t : P * (t + 1)].bitcast(FP8X4), lhsT_scale=w2s[:, P * t : P * (t + 1)],
-                                    rhs=gw[:, cols].bitcast(FP8X4), rhs_scale=gs[:, cols], start=True, stop=True)
+                                    rhs=picked(cols), rhs_scale=gs[:, cols], start=True, stop=True)
             copy(eng, hb[:, 4 * P * c : 4 * P * (c + 1)].rearrange("p (n t) -> p n t", t=4), bank[:].rearrange("p t n -> p n t"))
 
         def quant(c0, c1):
@@ -87,7 +99,7 @@ def tile_picked_lora_none_p_kernel(tc, x_words, x_scales, w1_words, w1_scales, w
 
         def own(dst, a, cols, start):
             nc.tensor.matmul_mx(out=dst, lhsT=w1w[:, 2 * P * a : 2 * P * (a + 1)].bitcast(FP4X4), lhsT_scale=ws[:, P * a : P * (a + 1)],
-                                rhs=gw[:, cols].bitcast(FP8X4), rhs_scale=gs[:, cols], start=start, stop=False)
+                                rhs=picked(cols), rhs_scale=gs[:, cols], start=start, stop=False)
 
         def adapter(dst, a, cols, stop):
             nc.tensor.matmul_mx(out=dst, lhsT=w3w[:, 2 * P * a : 2 * P * (a + 1)].bitcast(FP4X4), lhsT_scale=ws[:, N + P * a : N + P * (a + 1)],
@@ -107,32 +119,35 @@ def tile_picked_lora_none_p_kernel(tc, x_words, x_scales, w1_words, w1_scales, w
             copy(eng, res[:], bank[:, : 2 * w])
             nc.sync.dma_start(out=outv[:, :, P * c0 : P * c1], in_=res[:].rearrange("p (a n) -> p a n", a=2))
 
-        obank = [ops.tile([P, 512], F32, name=f"obank{g}") for g in range(4)]
+        obank = [ops.tile([P, 512], F32, name=f"obank{g}") for g in range(3)]
         spans = [(0, 2), (2, 4), (4, 6), (6, 7)]
-        for g in range(4):
-            narrow(own, spans[g][0], spans[g][1], obank[g])
         hidden(0, "s")
-        hidden(1, "v")
+        hidden(1, "s")
         hidden(2, "s")
         hidden(3, "v")
-        quant(0, 2)
         hidden(4, "s")
-        hidden(5, "s")
-        quant(2, 4)
+        narrow(own, 0, 2, obank[0])
+        quant(0, 2)
+        hidden(5, "v")
+        hidden(6, "s")
         narrow(adapter, 0, 2, obank[0])
-        hidden(6, "v")
+        quant(2, 4)
         hidden(7, "s")
+        narrow(own, 2, 4, obank[1])
         narrow(adapter, 2, 4, obank[1])
+        quant(4, 6)
+        narrow(own, 4, 6, obank[2])
+        narrow(adapter, 4, 6, obank[2])
+        leave(0, 2, "v", obank[0], "res0")
+        obank.append(hps.tile([P, 512], F32, name="hbank"))
+        narrow(own, 6, 7, obank[3])
         last = hps.tile([P, 512], F32, name="hbank")
         narrow(own, 7, 8, last)
-        quant(4, 6)
-        leave(0, 2, "s", obank[0], "res0")
         quant(6, 7)
         quant(7, 8)
-        narrow(adapter, 4, 6, obank[2])
         narrow(adapter, 6, 7, obank[3])
         narrow(adapter, 7, 8, last)
-        leave(2, 4, "v", obank[1], "res1")
-        leave(4, 6, "s", obank[2], "res2")
-        leave(6, 7, "v", obank[3], "res3")
+        leave(2, 4, "s", obank[1], "res1")
+        leave(4, 6, "v", obank[2], "res2")
+        leave(6, 7, "s", obank[3], "res3")
         leave(7, 8, "v", last, "res4")

@@ -13,141 +13,137 @@ U16 = mybir.dt.uint16
 U8 = mybir.dt.uint8
 FP8X4 = mybir.dt.float8_e4m3fn_x4
 FP4X4 = mybir.dt.float4_e2m1fn_x4
+
 P = 128
+PACK = 4
+BANK = 512
+LIST_ROWS = 16
+CHUNK = BANK // PACK
+GATHER = 2 * CHUNK
+M_TILES = N // P
+HELD_BANKS = 3
+TURN_BANKS = 5
 
 
 def tile_picked_lora_none_p_kernel(tc, x_words, x_scales, w1_words, w1_scales, w2, w3_words, w3_scales, offs, out):
     nc = tc.nc
     with ExitStack() as ctx:
         keep = ctx.enter_context(tc.tile_pool(name="keep", bufs=1))
-        hps = ctx.enter_context(tc.psum_pool(name="hps", bufs=5))
-        ops = ctx.enter_context(tc.psum_pool(name="ops", bufs=1))
+        turn = ctx.enter_context(tc.psum_pool(name="turn", bufs=TURN_BANKS))
+        held = ctx.enter_context(tc.psum_pool(name="held", bufs=1))
 
-        offsets = keep.tile([P, S // 16], U16, name="offsets")
-        nc.sync.dma_start(offsets[:], offs)
-
-        w2v = w2.rearrange("(p j) c -> p j c", j=4)
-        w2raw = [keep.tile([P, 4, H // 2], F32, name=f"w2raw{u}") for u in range(2)]
-        nc.sync.dma_start(out=w2raw[0][:], in_=w2v[:, :, : H // 2])
-        xs = keep.tile([P, T], U8, name="xs", tag="xs", align_bytes=64)
-        nc.vector.memset(xs[:].bitcast(I32), 0)
-        ws = keep.tile([P, 2 * N], U8, name="ws", align_bytes=64)
-        nc.vector.memset(ws[:].bitcast(I32), 0)
-        for q in range(4):
-            nc.sync.dma_start(out=xs[32 * q : 32 * q + 4, :].bitcast(I32), in_=x_scales[0, 4 * q : 4 * q + 4, :].bitcast(I32))
-        nc.sync.dma_start(out=w2raw[1][:], in_=w2v[:, :, H // 2 :])
-        xw = keep.tile([P, T], I32, name="xw", align_bytes=64)
-        nc.sync.dma_start(out=xw[:], in_=x_words[0].rearrange("p n t -> p (n t)").bitcast(I32))
-        w1w = keep.tile([P, 2 * N], U8, name="w1w", align_bytes=64)
-        w3w = keep.tile([P, 2 * N], U8, name="w3w", align_bytes=64)
-        for a, (wt, wd, sc) in enumerate(((w1w, w1_words, w1_scales), (w3w, w3_words, w3_scales))):
-            nc.sync.dma_start(out=wt[:].bitcast(I32), in_=wd[0].bitcast(I32))
+        def load_scale_rows(dst, rows):
             for q in range(4):
-                nc.sync.dma_start(out=ws[32 * q : 32 * q + 4, a * N : (a + 1) * N].bitcast(I32), in_=sc[0, 4 * q : 4 * q + 4, :].bitcast(I32))
+                nc.sync.dma_start(out=dst[32 * q : 32 * q + 4, :].bitcast(I32), in_=rows[4 * q : 4 * q + 4, :].bitcast(I32))
 
-        zb = keep.tile([P, 4 * 512], BF16, name="zb", align_bytes=64)
-        nc.vector.memset(zb[:].bitcast(I32), 0)
-        zq = keep.tile([P, 512], U32, name="zq", align_bytes=64)
-        zs = keep.tile([P, 512], U8, name="zs", align_bytes=64)
-        nc.vector.quantize_mx(out=zq[:].bitcast(FP8X4), scales=zs[:], in_=zb[:])
+        offsets = keep.tile([P, S // LIST_ROWS], U16, name="offsets")
+        w2_rows = w2.rearrange("(p j) c -> p j c", j=PACK)
+        w2_raw = [keep.tile([P, PACK, H // 2], F32, name=f"w2_raw{u}") for u in range(2)]
+        nc.sync.dma_start(out=w2_raw[0][:], in_=w2_rows[:, :, : H // 2])
+        nc.sync.dma_start(offsets[:], offs)
+        x_scale = keep.tile([P, T], U8, name="x_scale", tag="x_scale_then_w2_word", align_bytes=64)
+        nc.vector.memset(x_scale[:].bitcast(I32), 0)
+        w_scale = keep.tile([P, 2 * N], U8, name="w_scale", align_bytes=64)
+        nc.vector.memset(w_scale[:].bitcast(I32), 0)
+        load_scale_rows(x_scale, x_scales[0])
+        nc.sync.dma_start(out=w2_raw[1][:], in_=w2_rows[:, :, H // 2 :])
+        x_word = keep.tile([P, T], I32, name="x_word", align_bytes=64)
+        nc.sync.dma_start(out=x_word[:], in_=x_words[0].rearrange("p n t -> p (n t)").bitcast(I32))
+        w1_word = keep.tile([P, 2 * N], U8, name="w1_word", align_bytes=64)
+        w3_word = keep.tile([P, 2 * N], U8, name="w3_word", align_bytes=64)
+        nc.sync.dma_start(out=w1_word[:].bitcast(I32), in_=w1_words[0].bitcast(I32))
+        load_scale_rows(w_scale[:, :N], w1_scales[0])
+        nc.sync.dma_start(out=w3_word[:].bitcast(I32), in_=w3_words[0].bitcast(I32))
+        load_scale_rows(w_scale[:, N:], w3_scales[0])
 
-        gs = keep.tile([P, S], U8, name="gs", align_bytes=64)
+        picked_scale = keep.tile([P, S], U8, name="picked_scale", align_bytes=64)
         for u in range(2):
-            nc.vector.tensor_copy(gs[:, 512 * u : 512 * (u + 1)], xs[:].indirect(offsets[:, 32 * u : 32 * (u + 1)]))
-        for u in range(4):
-            warm = hps.tile([P, 512], F32, name="hbank")
-            nc.tensor.matmul_mx(out=warm[:], lhsT=zq[:, :P].bitcast(FP8X4), lhsT_scale=zs[:, :P],
-                                rhs=zq[:].bitcast(FP8X4), rhs_scale=gs[:, :512], start=True, stop=True)
+            entries = offsets[:, u * BANK // LIST_ROWS : (u + 1) * BANK // LIST_ROWS]
+            nc.vector.tensor_copy(picked_scale[:, u * BANK : (u + 1) * BANK], x_scale[:].indirect(entries))
 
-        w2b = keep.tile([P, 4, P, 4], BF16, name="w2b", tag="w2b", align_bytes=64)
-        dst = w2b[:].rearrange("p t m j -> p m j t")
+        w2_bf = keep.tile([P, PACK, P, PACK], BF16, name="w2_bf", tag="w2_bf_then_picked_word", align_bytes=64)
+        w2_dealt = w2_bf[:].rearrange("p t m j -> p m j t")
         for u in range(2):
-            nc.scalar.copy(out=dst[:, 64 * u : 64 * (u + 1)], in_=w2raw[u][:].rearrange("p j (m t) -> p m j t", t=4))
-        w2q = keep.tile([P, H], U32, name="w2q", tag="xs", align_bytes=64)
-        w2s = keep.tile([P, H], U8, name="w2s", align_bytes=64)
-        nc.vector.quantize_mx(out=w2q[:].bitcast(FP8X4), scales=w2s[:], in_=w2b[:].rearrange("p t m j -> p (t m j)"))
+            nc.scalar.copy(out=w2_dealt[:, u * P // 2 : (u + 1) * P // 2], in_=w2_raw[u][:].rearrange("p j (m t) -> p m j t", t=PACK))
+        w2_word = keep.tile([P, H], U32, name="w2_word", tag="x_scale_then_w2_word", align_bytes=64)
+        w2_scale = keep.tile([P, H], U8, name="w2_scale", align_bytes=64)
+        nc.vector.quantize_mx(out=w2_word[:].bitcast(FP8X4), scales=w2_scale[:], in_=w2_bf[:].rearrange("p t m j -> p (t m j)"))
 
-        gw = keep.tile([P, S], U32, name="gw", tag="w2b", align_bytes=64)
-        for g in range(4):
-            nc.vector.tensor_copy(gw[:, 256 * g : 256 * (g + 1)], xw[:].bitcast(U32).indirect(offsets[:, 16 * g : 16 * (g + 1)]))
+        picked_word = keep.tile([P, S], U32, name="picked_word", tag="w2_bf_then_picked_word", align_bytes=64)
+        for g in range(S // GATHER):
+            entries = offsets[:, g * GATHER // LIST_ROWS : (g + 1) * GATHER // LIST_ROWS]
+            nc.vector.tensor_copy(picked_word[:, g * GATHER : (g + 1) * GATHER], x_word[:].bitcast(U32).indirect(entries))
 
-        def picked(cols):
-            return gw[:, cols].bitcast(FP8X4)
+        h_bf = keep.tile([P, S * PACK], BF16, name="h_bf", align_bytes=64)
+        h_word = keep.tile([P, S], U32, name="h_word", align_bytes=64)
+        h_scale = keep.tile([P, S], U8, name="h_scale", align_bytes=64)
+        out_tiles = out.rearrange("(a p) n -> p a n", p=P)
+        on_scalar, on_vector = nc.scalar.copy, nc.vector.tensor_copy
 
-        hb = keep.tile([P, S * 4], BF16, name="hb", align_bytes=64)
-        hq = keep.tile([P, S], U32, name="hq", align_bytes=64)
-        hs = keep.tile([P, S], U8, name="hs", align_bytes=64)
-        outv = out.rearrange("(a p) n -> p a n", p=P)
+        def tokens(first, last):
+            return slice(CHUNK * first, CHUNK * last)
 
-        def copy(eng, dst, src):
-            if eng == "s":
-                nc.scalar.copy(out=dst, in_=src)
-            else:
-                nc.vector.tensor_copy(out=dst, in_=src)
+        def hidden(c, copy):
+            cols = tokens(c, c + 1)
+            bank = turn.tile([P, PACK, CHUNK], F32, name="bank")
+            for t in range(PACK):
+                nc.tensor.matmul_mx(out=bank[:, t, :], lhsT=w2_word[:, P * t : P * (t + 1)].bitcast(FP8X4), lhsT_scale=w2_scale[:, P * t : P * (t + 1)],
+                                    rhs=picked_word[:, cols].bitcast(FP8X4), rhs_scale=picked_scale[:, cols], start=True, stop=True)
+            copy(out=h_bf[:, PACK * cols.start : PACK * cols.stop].rearrange("p (n t) -> p n t", t=PACK), in_=bank[:].rearrange("p t n -> p n t"))
 
-        def hidden(c, eng):
-            cols = slice(P * c, P * (c + 1))
-            bank = hps.tile([P, 4, P], F32, name="hbank")
-            for t in range(4):
-                nc.tensor.matmul_mx(out=bank[:, t, :], lhsT=w2q[:, P * t : P * (t + 1)].bitcast(FP8X4), lhsT_scale=w2s[:, P * t : P * (t + 1)],
-                                    rhs=picked(cols), rhs_scale=gs[:, cols], start=True, stop=True)
-            copy(eng, hb[:, 4 * P * c : 4 * P * (c + 1)].rearrange("p (n t) -> p n t", t=4), bank[:].rearrange("p t n -> p n t"))
+        def quantise(first, last):
+            cols = tokens(first, last)
+            nc.vector.quantize_mx(out=h_word[:, cols].bitcast(FP8X4), scales=h_scale[:, cols], in_=h_bf[:, PACK * cols.start : PACK * cols.stop])
 
-        def quant(c0, c1):
-            cols = slice(P * c0, P * c1)
-            nc.vector.quantize_mx(out=hq[:, cols].bitcast(FP8X4), scales=hs[:, cols], in_=hb[:, 4 * P * c0 : 4 * P * c1])
+        def term(bank, first, last, w_word, scale_col, words, scales, opens):
+            width = CHUNK * (last - first)
+            passes = [(c, a) for c in range(first, last) for a in range(M_TILES)]
+            for c, a in passes:
+                col = a * width + CHUNK * (c - first)
+                nc.tensor.matmul_mx(out=bank[:, col : col + CHUNK], lhsT=w_word[:, 2 * P * a : 2 * P * (a + 1)].bitcast(FP4X4),
+                                    lhsT_scale=w_scale[:, scale_col + P * a : scale_col + P * (a + 1)],
+                                    rhs=words[:, tokens(c, c + 1)].bitcast(FP8X4), rhs_scale=scales[:, tokens(c, c + 1)],
+                                    start=opens and (c, a) == passes[0], stop=not opens and (c, a) == passes[-1])
 
-        def own(dst, a, cols, start):
-            nc.tensor.matmul_mx(out=dst, lhsT=w1w[:, 2 * P * a : 2 * P * (a + 1)].bitcast(FP4X4), lhsT_scale=ws[:, P * a : P * (a + 1)],
-                                rhs=picked(cols), rhs_scale=gs[:, cols], start=start, stop=False)
+        def own_term(bank, first, last):
+            term(bank, first, last, w1_word, 0, picked_word, picked_scale, True)
 
-        def adapter(dst, a, cols, stop):
-            nc.tensor.matmul_mx(out=dst, lhsT=w3w[:, 2 * P * a : 2 * P * (a + 1)].bitcast(FP4X4), lhsT_scale=ws[:, N + P * a : N + P * (a + 1)],
-                                rhs=hq[:, cols].bitcast(FP8X4), rhs_scale=hs[:, cols], start=False, stop=stop)
+        def adapter_term(bank, first, last):
+            term(bank, first, last, w3_word, N, h_word, h_scale, False)
 
-        def narrow(fn, c0, c1, bank):
-            w = P * (c1 - c0)
-            for c in range(c0, c1):
-                for a in range(2):
-                    dst = bank[:, a * w + P * (c - c0) : a * w + P * (c - c0 + 1)]
-                    edge = (c == c0 and a == 0) if fn is own else (c == c1 - 1 and a == 1)
-                    fn(dst, a, slice(P * c, P * (c + 1)), edge)
+        def store(bank, first, last, copy):
+            width = CHUNK * (last - first)
+            result = keep.tile([P, M_TILES * width], F32, name=f"result{first}")
+            copy(out=result[:], in_=bank[:, : M_TILES * width])
+            nc.sync.dma_start(out=out_tiles[:, :, tokens(first, last)], in_=result[:].rearrange("p (a n) -> p a n", a=M_TILES))
 
-        def leave(c0, c1, eng, bank, name):
-            w = P * (c1 - c0)
-            res = keep.tile([P, 2 * w], F32, name=name)
-            copy(eng, res[:], bank[:, : 2 * w])
-            nc.sync.dma_start(out=outv[:, :, P * c0 : P * c1], in_=res[:].rearrange("p (a n) -> p a n", a=2))
-
-        obank = [ops.tile([P, 512], F32, name=f"obank{g}") for g in range(3)]
-        spans = [(0, 2), (2, 4), (4, 6), (6, 7)]
-        hidden(0, "s")
-        hidden(1, "s")
-        hidden(2, "s")
-        hidden(3, "v")
-        hidden(4, "s")
-        narrow(own, 0, 2, obank[0])
-        quant(0, 2)
-        hidden(5, "v")
-        hidden(6, "s")
-        narrow(adapter, 0, 2, obank[0])
-        quant(2, 4)
-        hidden(7, "s")
-        narrow(own, 2, 4, obank[1])
-        narrow(adapter, 2, 4, obank[1])
-        quant(4, 6)
-        narrow(own, 4, 6, obank[2])
-        narrow(adapter, 4, 6, obank[2])
-        leave(0, 2, "v", obank[0], "res0")
-        obank.append(hps.tile([P, 512], F32, name="hbank"))
-        narrow(own, 6, 7, obank[3])
-        last = hps.tile([P, 512], F32, name="hbank")
-        narrow(own, 7, 8, last)
-        quant(6, 7)
-        quant(7, 8)
-        narrow(adapter, 6, 7, obank[3])
-        narrow(adapter, 7, 8, last)
-        leave(2, 4, "s", obank[1], "res1")
-        leave(4, 6, "v", obank[2], "res2")
-        leave(6, 7, "s", obank[3], "res3")
-        leave(7, 8, "v", last, "res4")
+        out_bank = [held.tile([P, BANK], F32, name=f"out_bank{g}") for g in range(HELD_BANKS)]
+        hidden(0, on_scalar)
+        hidden(1, on_scalar)
+        hidden(2, on_scalar)
+        hidden(3, on_vector)
+        hidden(4, on_scalar)
+        own_term(out_bank[0], 0, 2)
+        quantise(0, 2)
+        hidden(5, on_vector)
+        hidden(6, on_scalar)
+        adapter_term(out_bank[0], 0, 2)
+        quantise(2, 4)
+        quantise(4, 6)
+        hidden(7, on_vector)
+        own_term(out_bank[1], 2, 4)
+        adapter_term(out_bank[1], 2, 4)
+        store(out_bank[0], 0, 2, on_scalar)
+        own_term(out_bank[2], 4, 6)
+        adapter_term(out_bank[2], 4, 6)
+        tail = [(c, turn.tile([P, BANK], F32, name="bank")) for c in (6, 7)]
+        for c, bank in tail:
+            own_term(bank, c, c + 1)
+        for c, bank in tail:
+            quantise(c, c + 1)
+        for c, bank in tail:
+            adapter_term(bank, c, c + 1)
+        store(out_bank[1], 2, 4, on_scalar)
+        store(out_bank[2], 4, 6, on_vector)
+        for (c, bank), copy in zip(tail, (on_scalar, on_vector)):
+            store(bank, c, c + 1, copy)

@@ -23,6 +23,7 @@ GATHER = 2 * CHUNK
 M_TILES = N // P
 HELD_BANKS = 3
 TURN_BANKS = 5
+WARM_PASSES = 4
 
 
 def tile_picked_lora_none_p_kernel(tc, x_words, x_scales, w1_words, w1_scales, w2, w3_words, w3_scales, offs, out):
@@ -56,10 +57,21 @@ def tile_picked_lora_none_p_kernel(tc, x_words, x_scales, w1_words, w1_scales, w
         nc.sync.dma_start(out=w3_word[:].bitcast(I32), in_=w3_words[0].bitcast(I32))
         load_scale_rows(w_scale[:, N:], w3_scales[0])
 
+        zero = keep.tile([P, PACK * BANK], BF16, name="zero", align_bytes=64)
+        nc.vector.memset(zero[:].bitcast(I32), 0)
+        zero_word = keep.tile([P, BANK], U32, name="zero_word", align_bytes=64)
+        zero_scale = keep.tile([P, BANK], U8, name="zero_scale", align_bytes=64)
+        nc.vector.quantize_mx(out=zero_word[:].bitcast(FP8X4), scales=zero_scale[:], in_=zero[:])
+
         picked_scale = keep.tile([P, S], U8, name="picked_scale", align_bytes=64)
         for u in range(2):
             entries = offsets[:, u * BANK // LIST_ROWS : (u + 1) * BANK // LIST_ROWS]
             nc.vector.tensor_copy(picked_scale[:, u * BANK : (u + 1) * BANK], x_scale[:].indirect(entries))
+
+        for u in range(WARM_PASSES):
+            warm = turn.tile([P, BANK], F32, name="bank")
+            nc.tensor.matmul_mx(out=warm[:], lhsT=zero_word[:, :P].bitcast(FP8X4), lhsT_scale=zero_scale[:, :P],
+                                rhs=zero_word[:].bitcast(FP8X4), rhs_scale=picked_scale[:, :BANK], start=True, stop=True)
 
         w2_bf = keep.tile([P, PACK, P, PACK], BF16, name="w2_bf", tag="w2_bf_then_picked_word", align_bytes=64)
         w2_dealt = w2_bf[:].rearrange("p t m j -> p m j t")

from contextlib import ExitStack

import concourse.mybir as mybir

K, T, S, H, N = 512, 2048, 1024, 512, 256
FLOPS = 2 * S * (K * H + K * N + H * N)

F32 = mybir.dt.float32
BF16 = mybir.dt.bfloat16
I32 = mybir.dt.int32
U32 = mybir.dt.uint32
U16 = mybir.dt.uint16
U8 = mybir.dt.uint8
FP8X4 = mybir.dt.float8_e4m3fn_x4
FP4X4 = mybir.dt.float4_e2m1fn_x4

P = 128
PACK = 4
BANK = 512
LIST_ROWS = 16
CHUNK = BANK // PACK
GATHER = 2 * CHUNK
M_TILES = N // P
HELD_BANKS = 3
TURN_BANKS = 5
WARM_PASSES = 4


def tile_picked_lora_none_p_kernel(tc, x_words, x_scales, w1_words, w1_scales, w2, w3_words, w3_scales, offs, out):
    nc = tc.nc
    with ExitStack() as ctx:
        keep = ctx.enter_context(tc.tile_pool(name="keep", bufs=1))
        turn = ctx.enter_context(tc.psum_pool(name="turn", bufs=TURN_BANKS))
        held = ctx.enter_context(tc.psum_pool(name="held", bufs=1))

        def load_scale_rows(dst, rows):
            for q in range(4):
                nc.sync.dma_start(out=dst[32 * q : 32 * q + 4, :].bitcast(I32), in_=rows[4 * q : 4 * q + 4, :].bitcast(I32))

        offsets = keep.tile([P, S // LIST_ROWS], U16, name="offsets")
        w2_rows = w2.rearrange("(p j) c -> p j c", j=PACK)
        w2_raw = [keep.tile([P, PACK, H // 2], F32, name=f"w2_raw{u}") for u in range(2)]
        nc.sync.dma_start(out=w2_raw[0][:], in_=w2_rows[:, :, : H // 2])
        nc.sync.dma_start(offsets[:], offs)
        x_scale = keep.tile([P, T], U8, name="x_scale", tag="x_scale_then_w2_word", align_bytes=64)
        nc.vector.memset(x_scale[:].bitcast(I32), 0)
        w_scale = keep.tile([P, 2 * N], U8, name="w_scale", align_bytes=64)
        nc.vector.memset(w_scale[:].bitcast(I32), 0)
        load_scale_rows(x_scale, x_scales[0])
        nc.sync.dma_start(out=w2_raw[1][:], in_=w2_rows[:, :, H // 2 :])
        x_word = keep.tile([P, T], I32, name="x_word", align_bytes=64)
        nc.sync.dma_start(out=x_word[:], in_=x_words[0].rearrange("p n t -> p (n t)").bitcast(I32))
        w1_word = keep.tile([P, 2 * N], U8, name="w1_word", align_bytes=64)
        w3_word = keep.tile([P, 2 * N], U8, name="w3_word", align_bytes=64)
        nc.sync.dma_start(out=w1_word[:].bitcast(I32), in_=w1_words[0].bitcast(I32))
        load_scale_rows(w_scale[:, :N], w1_scales[0])
        nc.sync.dma_start(out=w3_word[:].bitcast(I32), in_=w3_words[0].bitcast(I32))
        load_scale_rows(w_scale[:, N:], w3_scales[0])

        zero = keep.tile([P, PACK * BANK], BF16, name="zero", align_bytes=64)
        nc.vector.memset(zero[:].bitcast(I32), 0)
        zero_word = keep.tile([P, BANK], U32, name="zero_word", align_bytes=64)
        zero_scale = keep.tile([P, BANK], U8, name="zero_scale", align_bytes=64)
        nc.vector.quantize_mx(out=zero_word[:].bitcast(FP8X4), scales=zero_scale[:], in_=zero[:])

        picked_scale = keep.tile([P, S], U8, name="picked_scale", align_bytes=64)
        for u in range(2):
            entries = offsets[:, u * BANK // LIST_ROWS : (u + 1) * BANK // LIST_ROWS]
            nc.vector.tensor_copy(picked_scale[:, u * BANK : (u + 1) * BANK], x_scale[:].indirect(entries))

        for u in range(WARM_PASSES):
            warm = turn.tile([P, BANK], F32, name="bank")
            nc.tensor.matmul_mx(out=warm[:], lhsT=zero_word[:, :P].bitcast(FP8X4), lhsT_scale=zero_scale[:, :P],
                                rhs=zero_word[:].bitcast(FP8X4), rhs_scale=picked_scale[:, :BANK], start=True, stop=True)

        w2_bf = keep.tile([P, PACK, P, PACK], BF16, name="w2_bf", tag="w2_bf_then_picked_word", align_bytes=64)
        w2_dealt = w2_bf[:].rearrange("p t m j -> p m j t")
        for u in range(2):
            nc.scalar.copy(out=w2_dealt[:, u * P // 2 : (u + 1) * P // 2], in_=w2_raw[u][:].rearrange("p j (m t) -> p m j t", t=PACK))
        w2_word = keep.tile([P, H], U32, name="w2_word", tag="x_scale_then_w2_word", align_bytes=64)
        w2_scale = keep.tile([P, H], U8, name="w2_scale", align_bytes=64)
        nc.vector.quantize_mx(out=w2_word[:].bitcast(FP8X4), scales=w2_scale[:], in_=w2_bf[:].rearrange("p t m j -> p (t m j)"))

        picked_word = keep.tile([P, S], U32, name="picked_word", tag="w2_bf_then_picked_word", align_bytes=64)
        for g in range(S // GATHER):
            entries = offsets[:, g * GATHER // LIST_ROWS : (g + 1) * GATHER // LIST_ROWS]
            nc.vector.tensor_copy(picked_word[:, g * GATHER : (g + 1) * GATHER], x_word[:].bitcast(U32).indirect(entries))

        h_bf = keep.tile([P, S * PACK], BF16, name="h_bf", align_bytes=64)
        h_word = keep.tile([P, S], U32, name="h_word", align_bytes=64)
        h_scale = keep.tile([P, S], U8, name="h_scale", align_bytes=64)
        out_tiles = out.rearrange("(a p) n -> p a n", p=P)
        on_scalar, on_vector = nc.scalar.copy, nc.vector.tensor_copy

        def tokens(first, last):
            return slice(CHUNK * first, CHUNK * last)

        def hidden(c, copy):
            cols = tokens(c, c + 1)
            bank = turn.tile([P, PACK, CHUNK], F32, name="bank")
            for t in range(PACK):
                nc.tensor.matmul_mx(out=bank[:, t, :], lhsT=w2_word[:, P * t : P * (t + 1)].bitcast(FP8X4), lhsT_scale=w2_scale[:, P * t : P * (t + 1)],
                                    rhs=picked_word[:, cols].bitcast(FP8X4), rhs_scale=picked_scale[:, cols], start=True, stop=True)
            copy(out=h_bf[:, PACK * cols.start : PACK * cols.stop].rearrange("p (n t) -> p n t", t=PACK), in_=bank[:].rearrange("p t n -> p n t"))

        def quantise(first, last):
            cols = tokens(first, last)
            nc.vector.quantize_mx(out=h_word[:, cols].bitcast(FP8X4), scales=h_scale[:, cols], in_=h_bf[:, PACK * cols.start : PACK * cols.stop])

        def term(bank, first, last, w_word, scale_col, words, scales, opens):
            width = CHUNK * (last - first)
            passes = [(c, a) for c in range(first, last) for a in range(M_TILES)]
            for c, a in passes:
                col = a * width + CHUNK * (c - first)
                nc.tensor.matmul_mx(out=bank[:, col : col + CHUNK], lhsT=w_word[:, 2 * P * a : 2 * P * (a + 1)].bitcast(FP4X4),
                                    lhsT_scale=w_scale[:, scale_col + P * a : scale_col + P * (a + 1)],
                                    rhs=words[:, tokens(c, c + 1)].bitcast(FP8X4), rhs_scale=scales[:, tokens(c, c + 1)],
                                    start=opens and (c, a) == passes[0], stop=not opens and (c, a) == passes[-1])

        def own_term(bank, first, last):
            term(bank, first, last, w1_word, 0, picked_word, picked_scale, True)

        def adapter_term(bank, first, last):
            term(bank, first, last, w3_word, N, h_word, h_scale, False)

        def store(bank, first, last, copy):
            width = CHUNK * (last - first)
            result = keep.tile([P, M_TILES * width], F32, name=f"result{first}")
            copy(out=result[:], in_=bank[:, : M_TILES * width])
            nc.sync.dma_start(out=out_tiles[:, :, tokens(first, last)], in_=result[:].rearrange("p (a n) -> p a n", a=M_TILES))

        out_bank = [held.tile([P, BANK], F32, name=f"out_bank{g}") for g in range(HELD_BANKS)]
        hidden(0, on_scalar)
        hidden(1, on_scalar)
        hidden(2, on_scalar)
        hidden(3, on_vector)
        hidden(4, on_scalar)
        own_term(out_bank[0], 0, 2)
        quantise(0, 2)
        hidden(5, on_vector)
        hidden(6, on_scalar)
        adapter_term(out_bank[0], 0, 2)
        quantise(2, 4)
        quantise(4, 6)
        hidden(7, on_vector)
        own_term(out_bank[1], 2, 4)
        adapter_term(out_bank[1], 2, 4)
        store(out_bank[0], 0, 2, on_scalar)
        own_term(out_bank[2], 4, 6)
        adapter_term(out_bank[2], 4, 6)
        tail = [(c, turn.tile([P, BANK], F32, name="bank")) for c in (6, 7)]
        for c, bank in tail:
            own_term(bank, c, c + 1)
        for c, bank in tail:
            quantise(c, c + 1)
        for c, bank in tail:
            adapter_term(bank, c, c + 1)
        store(out_bank[1], 2, 4, on_scalar)
        store(out_bank[2], 4, 6, on_vector)
        for (c, bank), copy in zip(tail, (on_scalar, on_vector)):
            store(bank, c, c + 1, copy)
